import numpy as np, ml_dtypes
CORES = [24,26,29,31,48,50,53,55]
N = 8
import mx_ref
NC = 256
BF = ml_dtypes.bfloat16
def setup_inputs(rng):
    def f(*shape):
        return mx_ref.flush((rng.standard_normal(shape, dtype=np.float32) * np.exp2(rng.integers(-2, 3, shape[:-1] + (1,)))).astype(BF))
    return {"w": f(N, 128, 512), "x": f(N, 128, 4 * NC)}
def setup_inputs_blocks(rng):
    d = setup_inputs(rng)
    for k in ("w", "x"): d[k] = mx_ref.spread(d[k], rng, 4)
    return d
def setup_inputs_wide(rng):
    d = setup_inputs(rng)
    for k in ("w", "x"): d[k] = mx_ref.flush((d[k].astype(np.float32) * np.exp2(rng.integers(-8, 9, (N, 1, 1))).astype(np.float32)).astype(BF))
    return d
def setup_inputs_zeros(rng):
    d = setup_inputs(rng); v = d["x"].reshape(N, 128, -1, 4).copy()
    v[np.broadcast_to((rng.random((N, 1, v.shape[2], 1)) < 0.33), v.shape)] = 0
    d["x"] = v.reshape(d["x"].shape)
    return d
def reference(w, x):
    QX = [mx_ref.quantize(x[j]) for j in range(N)]
    y = np.zeros((N, 128, NC), np.float32)
    for r in range(N):
        qw = mx_ref.quantize(w[r])
        for j in range(N):
            p = mx_ref.matmul(qw, QX[j])
            y[r] = p if j == 0 else np.maximum(y[r], p)
    return {"y": y}

@@ -1,0 +1,160 @@
+from concourse.bass import DstId, RemoteDMATransfer
+from concourse.mybir import dt, AluOpType
+
+N = 8
+NC = 256
+NW = 128
+
+SCRATCH = {
+    "xb": ("sbuf", [128, 4 * NC], "bfloat16"),
+    "wb": ("sbuf", [128, 4 * NW], "bfloat16"),
+    "xq": ("sbuf", [128, N * NC], "float8_e4m3fn_x4"),
+    "xs": ("sbuf", [128, N * NC], "uint8"),
+    "wq": ("sbuf", [128, NW], "float8_e4m3fn_x4"),
+    "ws": ("sbuf", [128, NW], "uint8"),
+    "acc": ("sbuf", [128, NC], "float32"),
+    "ps": ("psum", [128, 512 * N], "float32"),
+}
+SEMAPHORES = (["ldx", "ldw", "qx", "qw", "vx", "st", "sent"]
+              + ["c%d" % j for j in range(N)] + ["s%d" % j for j in range(N)] + ["m%d" % j for j in range(N)])
+
+
+def _engines(mask):
+    return bin(mask).count("1")
+
+
+def _roles(cores, topo):
+    info = {}
+    for c in cores:
+        near = [d for d in cores if d != c and topo.chip(d) == topo.chip(c)]
+        far = [d for d in cores if topo.chip(d) != topo.chip(c)]
+        info[c] = {"near": near, "far": far, "port": all(topo.may_write(c, d) for d in far)}
+    for c in cores:
+        i = info[c]
+        i["mate"] = [d for d in i["near"] if topo.die(d) == topo.die(c)][0]
+        same = [d for d in i["far"] if topo.die(d) == topo.die(c)]
+        i["far_port"] = [d for d in same if info[d]["port"]][0]
+        i["far_inner"] = [d for d in same if not info[d]["port"]][0]
+        every = topo.mask(c, i["near"][0])
+        i["all"] = every
+        i["lo"] = every & topo.mask(c, i["far"][0])
+        i["hi"] = every & ~topo.mask(c, i["far"][0])
+    return info
+
+
+def _plan(cores, topo):
+    info = _roles(cores, topo)
+    rank = {c: j for j, c in enumerate(cores)}
+    plan = {}
+    for c in cores:
+        i, j = info[c], rank[c]
+        early, late = rank[i["far_port"]], rank[i["far_inner"]]
+        steps = [("wait", "qx")]
+        if i["port"]:
+            inner = rank[i["mate"]]
+            steps += [
+                ("send", [("c", j, [i["far_inner"]], i["lo"]), ("c", j, i["near"], i["hi"])]),
+                ("send", [("s", j, [i["far_port"]], i["lo"]), ("s", j, i["near"], i["hi"])]),
+                ("wait", "c%d" % inner), ("send", [("c", inner, [i["far_inner"]], i["lo"])]),
+                ("wait", "s%d" % inner), ("send", [("s", inner, [i["far_port"]], i["lo"])]),
+                ("wait", "s%d" % early), ("send", [("s", early, i["near"], i["all"])]),
+                ("wait", "s%d" % late), ("send", [("s", late, i["near"], i["all"])]),
+            ]
+        else:
+            rest = [d for d in i["near"] if d != i["mate"]]
+            steps += [
+                ("send", [("c", j, [i["mate"]], i["lo"])]),
+                ("send", [("s", j, [i["mate"]], i["hi"])]),
+                ("send", [("c", j, rest, i["all"])]),
+                ("send", [("s", j, rest, i["all"])]),
+                ("wait", "c%d" % early), ("send", [("c", early, i["near"], i["all"])]),
+                ("wait", "c%d" % late), ("send", [("c", late, i["near"], i["all"])]),
+            ]
+        plan[c] = steps
+    need = {}
+    for c in cores:
+        need[(c, "qx")] = 1
+        for step in plan[c]:
+            if step[0] == "send":
+                for kind, tile, dsts, mask in step[1]:
+                    for d in dsts:
+                        key = (d, "%s%d" % (kind, tile))
+                        need[key] = need.get(key, 0) + _engines(mask)
+    return info, plan, need
+
+
+def _view(T, kind, tile):
+    a = tile * NC
+    if kind == "c":
+        return T.xq[:, a:a + NC].bitcast(dt.uint8)
+    return T.xs[:, a:a + NC]
+
+
+def rank_program(g, core, T, topo):
+    me = T.rank_of(core)
+    if me is None:
+        return
+    cores = list(T.cores)
+    info, plan, need = _plan(cores, topo)
+    rank = {c: j for j, c in enumerate(cores)}
+    i = info[core]
+    sem = T.sem
+
+    g.sync.dma_start(T.xb[:], T.x[:]).then_inc(sem.ldx, 16)
+    g.sync.dma_start(T.wb[:], T.w[:]).then_inc(sem.ldw, 16)
+    a = me * NC
+    g.vector.wait_ge(sem.ldx, 16)
+    g.vector.quantize_mx(T.xq[:, a:a + NC], T.xs[:, a:a + NC], T.xb[:]).then_inc(sem.qx, 1)
+    g.vector.wait_ge(sem.ldw, 16)
+    g.vector.quantize_mx(T.wq[:], T.ws[:], T.wb[:]).then_inc(sem.qw, 1)
+
+    sent = 0
+    for step in plan[core]:
+        if step[0] == "wait":
+            g.wait_ge(sem[step[1]], need[(core, step[1])])
+            continue
+        parts = step[1]
+        sent += sum(_engines(mask) for _, _, _, mask in parts)
+        if len(parts) == 1 and len(parts[0][2]) == 1:
+            kind, tile, dsts, mask = parts[0]
+            rid, pid, _ = topo.addr(dsts[0])
+            g.remote_dma(_view(T, kind, tile), _view(T, kind, tile), sem["%s%d" % (kind, tile)], sem.sent,
+                         pid, rid, mask)
+            continue
+        transfers = []
+        for kind, tile, dsts, mask in parts:
+            ids = [DstId(rid=topo.addr(d)[0], pnc=topo.addr(d)[1]) for d in dsts]
+            transfers.append(RemoteDMATransfer(dst_ids=ids, dma_engine_mask=mask, remote_sem=sem["%s%d" % (kind, tile)],
+                                               srcs=[_view(T, kind, tile)], dsts=[_view(T, kind, tile) for _ in dsts]))
+        g.remote_dma_fused(transfers, local_sem=sem.sent)
+    g.wait_ge(sem.sent, sent)
+
+    other = [d for d in i["near"] if d != i["mate"]]
+    far_other = [d for d in i["far"] if topo.die(d) != topo.die(core)]
+    order = ([core, i["mate"]] + [d for d in other if not info[d]["port"]] + [d for d in other if info[d]["port"]]
+             + [i["far_port"]] + [d for d in far_other if info[d]["port"]]
+             + [i["far_inner"]] + [d for d in far_other if not info[d]["port"]])
+
+    g.tensor.wait_ge(sem.qw, 1)
+    g.tensor.wait_ge(sem.qx, 1)
+    for k, c in enumerate(order):
+        j = rank[c]
+        if c != core:
+            g.tensor.wait_ge(sem["c%d" % j], need[(core, "c%d" % j)])
+            g.tensor.wait_ge(sem["s%d" % j], need[(core, "s%d" % j)])
+        b = j * NC
+        g.tensor.matmul_mx(T.ps[:, 512 * k:512 * k + NC], T.wq[:], T.ws[:], T.xq[:, b:b + NC], T.xs[:, b:b + NC],
+                           True, True).then_inc(sem["m%d" % k], 1)
+
+    for k in range(N):
+        g.vector.wait_ge(sem["m%d" % k], 1)
+        bank = T.ps[:, 512 * k:512 * k + NC]
+        if k == 0:
+            g.vector.tensor_copy(T.acc[:], bank).then_inc(sem.vx, 1)
+        else:
+            g.vector.wait_ge(sem.vx, k)
+            g.vector.tensor_tensor(T.acc[:], bank, T.acc[:], AluOpType.max).then_inc(sem.vx, 1)
+
+    g.sync.wait_ge(sem.vx, N)
+    g.sync.dma_start(T.y[:], T.acc[:]).then_inc(sem.st, 16)
+    g.sync.wait_ge(sem.st, 16)

@@ -4,6 +4,7 @@ from concourse.mybir import dt, AluOpType
 N = 8
 NC = 256
 NW = 128
+NH = NC // 2
 
 SCRATCH = {
     "xb": ("sbuf", [128, 4 * NC], "bfloat16"),
@@ -15,8 +16,8 @@ SCRATCH = {
     "acc": ("sbuf", [128, NC], "float32"),
     "ps": ("psum", [128, 512 * N], "float32"),
 }
-SEMAPHORES = (["ldx", "ldw", "qx", "qw", "vx", "st", "sent"]
-              + ["c%d" % j for j in range(N)] + ["s%d" % j for j in range(N)] + ["m%d" % j for j in range(N)])
+SEMAPHORES = (["lda", "ldb", "ldw", "qa", "qb", "qw", "vx", "st", "sent"]
+              + ["c%d" % j for j in range(N)] + ["s%d" % j for j in range(N)] + ["m%d" % j for j in range(N + 1)])
 
 
 def _engines(mask):
@@ -32,6 +33,9 @@ def _roles(cores, topo):
     for c in cores:
         i = info[c]
         i["mate"] = [d for d in i["near"] if topo.die(d) == topo.die(c)][0]
+        rest = [d for d in i["near"] if d != i["mate"]]
+        i["rest"] = [d for d in rest if info[d]["port"]] + [d for d in rest if not info[d]["port"]]
+        i["near"] = [i["mate"]] + i["rest"]
         same = [d for d in i["far"] if topo.die(d) == topo.die(c)]
         i["far_port"] = [d for d in same if info[d]["port"]][0]
         i["far_inner"] = [d for d in same if not info[d]["port"]][0]
@@ -49,45 +53,48 @@ def _plan(cores, topo):
     for c in cores:
         i, j = info[c], rank[c]
         early, late = rank[i["far_port"]], rank[i["far_inner"]]
-        steps = [("wait", "qx")]
         if i["port"]:
             inner = rank[i["mate"]]
-            steps += [
-                ("send", [("c", j, [i["far_inner"]], i["lo"]), ("c", j, i["near"], i["hi"])]),
+            steps = [
+                ("wait", "qa"), ("send", [("ca", j, [i["far_inner"]], i["lo"])]),
+                ("wait", "qb"), ("send", [("cb", j, [i["far_inner"]], i["lo"])]),
                 ("send", [("s", j, [i["far_port"]], i["lo"]), ("s", j, i["near"], i["hi"])]),
+                ("send", [("c", j, i["near"], i["hi"])]),
                 ("wait", "c%d" % inner), ("send", [("c", inner, [i["far_inner"]], i["lo"])]),
                 ("wait", "s%d" % inner), ("send", [("s", inner, [i["far_port"]], i["lo"])]),
                 ("wait", "s%d" % early), ("send", [("s", early, i["near"], i["all"])]),
                 ("wait", "s%d" % late), ("send", [("s", late, i["near"], i["all"])]),
             ]
         else:
-            rest = [d for d in i["near"] if d != i["mate"]]
-            steps += [
-                ("send", [("c", j, [i["mate"]], i["lo"])]),
-                ("send", [("s", j, [i["mate"]], i["hi"])]),
-                ("send", [("c", j, rest, i["all"])]),
-                ("send", [("s", j, rest, i["all"])]),
+            steps = [
+                ("wait", "qa"), ("send", [("ca", j, [i["mate"]], i["lo"])]),
+                ("wait", "qb"), ("send", [("cb", j, [i["mate"]], i["hi"])]),
+                ("send", [("s", j, [i["mate"]], i["lo"])]),
+                ("send", [("c", j, i["rest"], i["all"])]),
+                ("send", [("s", j, i["rest"], i["all"])]),
                 ("wait", "c%d" % early), ("send", [("c", early, i["near"], i["all"])]),
                 ("wait", "c%d" % late), ("send", [("c", late, i["near"], i["all"])]),
             ]
         plan[c] = steps
     need = {}
     for c in cores:
-        need[(c, "qx")] = 1
+        need[(c, "qa")] = 1
+        need[(c, "qb")] = 1
         for step in plan[c]:
             if step[0] == "send":
                 for kind, tile, dsts, mask in step[1]:
                     for d in dsts:
-                        key = (d, "%s%d" % (kind, tile))
+                        key = (d, "%s%d" % (kind[0], tile))
                         need[key] = need.get(key, 0) + _engines(mask)
     return info, plan, need
 
 
 def _view(T, kind, tile):
     a = tile * NC
-    if kind == "c":
-        return T.xq[:, a:a + NC].bitcast(dt.uint8)
-    return T.xs[:, a:a + NC]
+    if kind == "s":
+        return T.xs[:, a:a + NC]
+    lo, hi = {"c": (0, NC), "ca": (0, NH), "cb": (NH, NC)}[kind]
+    return T.xq[:, a + lo:a + hi].bitcast(dt.uint8)
 
 
 def rank_program(g, core, T, topo):
@@ -100,11 +107,14 @@ def rank_program(g, core, T, topo):
     i = info[core]
     sem = T.sem
 
-    g.sync.dma_start(T.xb[:], T.x[:]).then_inc(sem.ldx, 16)
+    g.sync.dma_start(T.xb[:, 0:4 * NH], T.x[:, 0:4 * NH]).then_inc(sem.lda, 16)
+    g.sync.dma_start(T.xb[:, 4 * NH:4 * NC], T.x[:, 4 * NH:4 * NC]).then_inc(sem.ldb, 16)
     g.sync.dma_start(T.wb[:], T.w[:]).then_inc(sem.ldw, 16)
     a = me * NC
-    g.vector.wait_ge(sem.ldx, 16)
-    g.vector.quantize_mx(T.xq[:, a:a + NC], T.xs[:, a:a + NC], T.xb[:]).then_inc(sem.qx, 1)
+    g.vector.wait_ge(sem.lda, 16)
+    g.vector.quantize_mx(T.xq[:, a:a + NH], T.xs[:, a:a + NH], T.xb[:, 0:4 * NH]).then_inc(sem.qa, 1)
+    g.vector.wait_ge(sem.ldb, 16)
+    g.vector.quantize_mx(T.xq[:, a + NH:a + NC], T.xs[:, a + NH:a + NC], T.xb[:, 4 * NH:4 * NC]).then_inc(sem.qb, 1)
     g.vector.wait_ge(sem.ldw, 16)
     g.vector.quantize_mx(T.wq[:], T.ws[:], T.wb[:]).then_inc(sem.qw, 1)
 
@@ -118,35 +128,43 @@ def rank_program(g, core, T, topo):
         if len(parts) == 1 and len(parts[0][2]) == 1:
             kind, tile, dsts, mask = parts[0]
             rid, pid, _ = topo.addr(dsts[0])
-            g.remote_dma(_view(T, kind, tile), _view(T, kind, tile), sem["%s%d" % (kind, tile)], sem.sent,
+            g.remote_dma(_view(T, kind, tile), _view(T, kind, tile), sem["%s%d" % (kind[0], tile)], sem.sent,
                          pid, rid, mask)
             continue
         transfers = []
         for kind, tile, dsts, mask in parts:
             ids = [DstId(rid=topo.addr(d)[0], pnc=topo.addr(d)[1]) for d in dsts]
-            transfers.append(RemoteDMATransfer(dst_ids=ids, dma_engine_mask=mask, remote_sem=sem["%s%d" % (kind, tile)],
+            transfers.append(RemoteDMATransfer(dst_ids=ids, dma_engine_mask=mask,
+                                               remote_sem=sem["%s%d" % (kind[0], tile)],
                                                srcs=[_view(T, kind, tile)], dsts=[_view(T, kind, tile) for _ in dsts]))
         g.remote_dma_fused(transfers, local_sem=sem.sent)
     g.wait_ge(sem.sent, sent)
 
-    other = [d for d in i["near"] if d != i["mate"]]
     far_other = [d for d in i["far"] if topo.die(d) != topo.die(core)]
-    order = ([core, i["mate"]] + [d for d in other if not info[d]["port"]] + [d for d in other if info[d]["port"]]
+    order = ([core, i["mate"]] + i["rest"][::-1]
              + [i["far_port"]] + [d for d in far_other if info[d]["port"]]
              + [i["far_inner"]] + [d for d in far_other if not info[d]["port"]])
 
     g.tensor.wait_ge(sem.qw, 1)
-    g.tensor.wait_ge(sem.qx, 1)
+    g.tensor.wait_ge(sem.qa, 1)
+    g.tensor.wait_ge(sem.qb, 1)
     for k, c in enumerate(order):
         j = rank[c]
         if c != core:
             g.tensor.wait_ge(sem["c%d" % j], need[(core, "c%d" % j)])
             g.tensor.wait_ge(sem["s%d" % j], need[(core, "s%d" % j)])
         b = j * NC
-        g.tensor.matmul_mx(T.ps[:, 512 * k:512 * k + NC], T.wq[:], T.ws[:], T.xq[:, b:b + NC], T.xs[:, b:b + NC],
+        if k < N - 1:
+            g.tensor.matmul_mx(T.ps[:, 512 * k:512 * k + NC], T.wq[:], T.ws[:], T.xq[:, b:b + NC], T.xs[:, b:b + NC],
+                               True, True).then_inc(sem["m%d" % k], 1)
+            continue
+        g.tensor.matmul_mx(T.ps[:, 512 * k:512 * k + NH], T.wq[:], T.ws[:], T.xq[:, b:b + NH], T.xs[:, b:b + NH],
                            True, True).then_inc(sem["m%d" % k], 1)
+        g.tensor.wait_ge(sem.vx, 1)
+        g.tensor.matmul_mx(T.ps[:, 0:NH], T.wq[:], T.ws[:], T.xq[:, b + NH:b + NC], T.xs[:, b + NH:b + NC],
+                           True, True).then_inc(sem["m%d" % N], 1)
 
-    for k in range(N):
+    for k in range(N - 1):
         g.vector.wait_ge(sem["m%d" % k], 1)
         bank = T.ps[:, 512 * k:512 * k + NC]
         if k == 0:
@@ -154,7 +172,13 @@ def rank_program(g, core, T, topo):
         else:
             g.vector.wait_ge(sem.vx, k)
             g.vector.tensor_tensor(T.acc[:], bank, T.acc[:], AluOpType.max).then_inc(sem.vx, 1)
+    g.vector.wait_ge(sem["m%d" % (N - 1)], 1)
+    g.vector.wait_ge(sem.vx, N - 1)
+    g.vector.tensor_tensor(T.acc[:, 0:NH], T.ps[:, 512 * (N - 1):512 * (N - 1) + NH], T.acc[:, 0:NH],
+                           AluOpType.max).then_inc(sem.vx, 1)
+    g.vector.wait_ge(sem["m%d" % N], 1)
+    g.vector.tensor_tensor(T.acc[:, NH:NC], T.ps[:, 0:NH], T.acc[:, NH:NC], AluOpType.max).then_inc(sem.vx, 1)
 
-    g.sync.wait_ge(sem.vx, N)
+    g.sync.wait_ge(sem.vx, N + 1)
     g.sync.dma_start(T.y[:], T.acc[:]).then_inc(sem.st, 16)
     g.sync.wait_ge(sem.st, 16)

from concourse.bass import DstId, RemoteDMATransfer
from concourse.mybir import dt, AluOpType

N = 8
NC = 256
NW = 128
NH = NC // 2

SCRATCH = {
    "xb": ("sbuf", [128, 4 * NC], "bfloat16"),
    "wb": ("sbuf", [128, 4 * NW], "bfloat16"),
    "xq": ("sbuf", [128, N * NC], "float8_e4m3fn_x4"),
    "xs": ("sbuf", [128, N * NC], "uint8"),
    "wq": ("sbuf", [128, NW], "float8_e4m3fn_x4"),
    "ws": ("sbuf", [128, NW], "uint8"),
    "acc": ("sbuf", [128, NC], "float32"),
    "ps": ("psum", [128, 512 * N], "float32"),
}
SEMAPHORES = (["lda", "ldb", "ldw", "qa", "qb", "qw", "vx", "st", "sent"]
              + ["c%d" % j for j in range(N)] + ["s%d" % j for j in range(N)] + ["m%d" % j for j in range(N + 1)])


def _engines(mask):
    return bin(mask).count("1")


def _roles(cores, topo):
    info = {}
    for c in cores:
        near = [d for d in cores if d != c and topo.chip(d) == topo.chip(c)]
        far = [d for d in cores if topo.chip(d) != topo.chip(c)]
        info[c] = {"near": near, "far": far, "port": all(topo.may_write(c, d) for d in far)}
    for c in cores:
        i = info[c]
        i["mate"] = [d for d in i["near"] if topo.die(d) == topo.die(c)][0]
        rest = [d for d in i["near"] if d != i["mate"]]
        i["rest"] = [d for d in rest if info[d]["port"]] + [d for d in rest if not info[d]["port"]]
        i["near"] = [i["mate"]] + i["rest"]
        same = [d for d in i["far"] if topo.die(d) == topo.die(c)]
        i["far_port"] = [d for d in same if info[d]["port"]][0]
        i["far_inner"] = [d for d in same if not info[d]["port"]][0]
        every = topo.mask(c, i["near"][0])
        i["all"] = every
        i["lo"] = every & topo.mask(c, i["far"][0])
        i["hi"] = every & ~topo.mask(c, i["far"][0])
    return info


def _plan(cores, topo):
    info = _roles(cores, topo)
    rank = {c: j for j, c in enumerate(cores)}
    plan = {}
    for c in cores:
        i, j = info[c], rank[c]
        early, late = rank[i["far_port"]], rank[i["far_inner"]]
        if i["port"]:
            inner = rank[i["mate"]]
            steps = [
                ("wait", "qa"), ("send", [("ca", j, [i["far_inner"]], i["lo"])]),
                ("wait", "qb"), ("send", [("cb", j, [i["far_inner"]], i["lo"])]),
                ("send", [("s", j, [i["far_port"]], i["lo"]), ("s", j, i["near"], i["hi"])]),
                ("send", [("c", j, i["near"], i["hi"])]),
                ("wait", "c%d" % inner), ("send", [("c", inner, [i["far_inner"]], i["lo"])]),
                ("wait", "s%d" % inner), ("send", [("s", inner, [i["far_port"]], i["lo"])]),
                ("wait", "s%d" % early), ("send", [("s", early, i["near"], i["all"])]),
                ("wait", "s%d" % late), ("send", [("s", late, i["near"], i["all"])]),
            ]
        else:
            steps = [
                ("wait", "qa"), ("send", [("ca", j, [i["mate"]], i["lo"])]),
                ("wait", "qb"), ("send", [("cb", j, [i["mate"]], i["hi"])]),
                ("send", [("s", j, [i["mate"]], i["lo"])]),
                ("send", [("c", j, i["rest"], i["all"])]),
                ("send", [("s", j, i["rest"], i["all"])]),
                ("wait", "c%d" % early), ("send", [("c", early, i["near"], i["all"])]),
                ("wait", "c%d" % late), ("send", [("c", late, i["near"], i["all"])]),
            ]
        plan[c] = steps
    need = {}
    for c in cores:
        need[(c, "qa")] = 1
        need[(c, "qb")] = 1
        for step in plan[c]:
            if step[0] == "send":
                for kind, tile, dsts, mask in step[1]:
                    for d in dsts:
                        key = (d, "%s%d" % (kind[0], tile))
                        need[key] = need.get(key, 0) + _engines(mask)
    return info, plan, need


def _view(T, kind, tile):
    a = tile * NC
    if kind == "s":
        return T.xs[:, a:a + NC]
    lo, hi = {"c": (0, NC), "ca": (0, NH), "cb": (NH, NC)}[kind]
    return T.xq[:, a + lo:a + hi].bitcast(dt.uint8)


def rank_program(g, core, T, topo):
    me = T.rank_of(core)
    if me is None:
        return
    cores = list(T.cores)
    info, plan, need = _plan(cores, topo)
    rank = {c: j for j, c in enumerate(cores)}
    i = info[core]
    sem = T.sem

    g.sync.dma_start(T.xb[:, 0:4 * NH], T.x[:, 0:4 * NH]).then_inc(sem.lda, 16)
    g.sync.dma_start(T.xb[:, 4 * NH:4 * NC], T.x[:, 4 * NH:4 * NC]).then_inc(sem.ldb, 16)
    g.sync.dma_start(T.wb[:], T.w[:]).then_inc(sem.ldw, 16)
    a = me * NC
    g.vector.wait_ge(sem.lda, 16)
    g.vector.quantize_mx(T.xq[:, a:a + NH], T.xs[:, a:a + NH], T.xb[:, 0:4 * NH]).then_inc(sem.qa, 1)
    g.vector.wait_ge(sem.ldb, 16)
    g.vector.quantize_mx(T.xq[:, a + NH:a + NC], T.xs[:, a + NH:a + NC], T.xb[:, 4 * NH:4 * NC]).then_inc(sem.qb, 1)
    g.vector.wait_ge(sem.ldw, 16)
    g.vector.quantize_mx(T.wq[:], T.ws[:], T.wb[:]).then_inc(sem.qw, 1)

    sent = 0
    for step in plan[core]:
        if step[0] == "wait":
            g.wait_ge(sem[step[1]], need[(core, step[1])])
            continue
        parts = step[1]
        sent += sum(_engines(mask) for _, _, _, mask in parts)
        if len(parts) == 1 and len(parts[0][2]) == 1:
            kind, tile, dsts, mask = parts[0]
            rid, pid, _ = topo.addr(dsts[0])
            g.remote_dma(_view(T, kind, tile), _view(T, kind, tile), sem["%s%d" % (kind[0], tile)], sem.sent,
                         pid, rid, mask)
            continue
        transfers = []
        for kind, tile, dsts, mask in parts:
            ids = [DstId(rid=topo.addr(d)[0], pnc=topo.addr(d)[1]) for d in dsts]
            transfers.append(RemoteDMATransfer(dst_ids=ids, dma_engine_mask=mask,
                                               remote_sem=sem["%s%d" % (kind[0], tile)],
                                               srcs=[_view(T, kind, tile)], dsts=[_view(T, kind, tile) for _ in dsts]))
        g.remote_dma_fused(transfers, local_sem=sem.sent)
    g.wait_ge(sem.sent, sent)

    far_other = [d for d in i["far"] if topo.die(d) != topo.die(core)]
    order = ([core, i["mate"]] + i["rest"][::-1]
             + [i["far_port"]] + [d for d in far_other if info[d]["port"]]
             + [i["far_inner"]] + [d for d in far_other if not info[d]["port"]])

    g.tensor.wait_ge(sem.qw, 1)
    g.tensor.wait_ge(sem.qa, 1)
    g.tensor.wait_ge(sem.qb, 1)
    for k, c in enumerate(order):
        j = rank[c]
        if c != core:
            g.tensor.wait_ge(sem["c%d" % j], need[(core, "c%d" % j)])
            g.tensor.wait_ge(sem["s%d" % j], need[(core, "s%d" % j)])
        b = j * NC
        if k < N - 1:
            g.tensor.matmul_mx(T.ps[:, 512 * k:512 * k + NC], T.wq[:], T.ws[:], T.xq[:, b:b + NC], T.xs[:, b:b + NC],
                               True, True).then_inc(sem["m%d" % k], 1)
            continue
        g.tensor.matmul_mx(T.ps[:, 512 * k:512 * k + NH], T.wq[:], T.ws[:], T.xq[:, b:b + NH], T.xs[:, b:b + NH],
                           True, True).then_inc(sem["m%d" % k], 1)
        g.tensor.wait_ge(sem.vx, 1)
        g.tensor.matmul_mx(T.ps[:, 0:NH], T.wq[:], T.ws[:], T.xq[:, b + NH:b + NC], T.xs[:, b + NH:b + NC],
                           True, True).then_inc(sem["m%d" % N], 1)

    for k in range(N - 1):
        g.vector.wait_ge(sem["m%d" % k], 1)
        bank = T.ps[:, 512 * k:512 * k + NC]
        if k == 0:
            g.vector.tensor_copy(T.acc[:], bank).then_inc(sem.vx, 1)
        else:
            g.vector.wait_ge(sem.vx, k)
            g.vector.tensor_tensor(T.acc[:], bank, T.acc[:], AluOpType.max).then_inc(sem.vx, 1)
    g.vector.wait_ge(sem["m%d" % (N - 1)], 1)
    g.vector.wait_ge(sem.vx, N - 1)
    g.vector.tensor_tensor(T.acc[:, 0:NH], T.ps[:, 512 * (N - 1):512 * (N - 1) + NH], T.acc[:, 0:NH],
                           AluOpType.max).then_inc(sem.vx, 1)
    g.vector.wait_ge(sem["m%d" % N], 1)
    g.vector.tensor_tensor(T.acc[:, NH:NC], T.ps[:, 0:NH], T.acc[:, NH:NC], AluOpType.max).then_inc(sem.vx, 1)

    g.sync.wait_ge(sem.vx, N + 1)
    g.sync.dma_start(T.y[:], T.acc[:]).then_inc(sem.st, 16)
    g.sync.wait_ge(sem.st, 16)
